import numpy as np
import ml_dtypes


def mxq(x, axis, fmt="e4m3"):
    dtype, down = {"e4m3": (ml_dtypes.float8_e4m3fn, 7), "e5m2": (ml_dtypes.float8_e5m2, 14)}[fmt]
    v = np.moveaxis(np.asarray(x, np.float32).astype(ml_dtypes.bfloat16).astype(np.float64), axis, -1)
    blocks = v.reshape(v.shape[:-1] + (-1, 32))
    amax = np.abs(blocks).max(-1, keepdims=True)
    byte = np.maximum(np.where(amax > 0, np.frexp(amax)[1] - 1 + 127, 0) - down, 1)
    scale = np.exp2(byte - 127.0)
    codes = (blocks / scale).astype(np.float32).astype(dtype).astype(np.float64)
    return np.moveaxis((codes * scale).reshape(v.shape), -1, axis)


WIDE = False


def mx_kscale(k):
    if not WIDE:
        return np.ones(k)
    levels = np.array([10, -10, 5, -5, 0])
    if k % 512:
        return np.exp2(np.random.permutation(np.resize(levels, k // 32))).repeat(32)
    a = np.empty((k // 512, 16))
    for p in range(k // 512):
        a[p, :8] = np.random.permutation(np.resize(levels, 8))
        for g in range(8):
            far = levels[np.abs(levels - a[p, g]) >= 10]
            a[p, g + 8] = far[np.random.randint(len(far))]
    return np.exp2(a.ravel()).repeat(32)


def f64(x):
    return np.asarray(x).astype(np.float64)


def striped(idx):
    return np.tile(idx.reshape(-1, 16).T, (8, 1)).astype(np.uint16)


def unstriped(offs):
    return offs[:16].T.reshape(-1).astype(np.int64)


E2M1 = np.array([0.0, 0.5, 1.0, 1.5, 2.0, 3.0, 4.0, 6.0, -0.0, -0.5, -1.0, -1.5, -2.0, -3.0, -4.0, -6.0])


def pack_weight(w, fmt):
    k, n = w.shape
    w = f64(np.asarray(w, np.float32).astype(ml_dtypes.bfloat16)).reshape(k // 32, 32, n)
    amax = np.abs(w).max(1)
    if fmt == "e4m3":
        byte = np.frexp(amax)[1] - 1 + 127 - 7
    else:
        mant, ex = np.frexp(amax / 6.0)
        byte = np.where(mant > 0.5, ex, ex - 1) + 127
    byte = np.clip(np.where(amax > 0, byte, 1), 1, 254)
    scaled = (w * np.exp2(127.0 - byte)[:, None, :]).reshape(k, n).astype(np.float32)
    by_word = np.ascontiguousarray(scaled.reshape(k // 512, 128, 4, n).transpose(0, 1, 3, 2))
    if fmt == "e4m3":
        words = by_word.astype(ml_dtypes.float8_e4m3fn).view(np.uint8)
    else:
        c = by_word.astype(ml_dtypes.float4_e2m1fn).view(np.uint8) & 0xF
        words = (c[..., 0::2] | (c[..., 1::2] << 4)).reshape(k // 512, 128, 2 * n)
    return np.ascontiguousarray(words), np.ascontiguousarray(byte.astype(np.uint8).reshape(k // 512, 16, n))


def unpack_weight(words, scales, fmt):
    g, _, n = scales.shape
    words = np.ascontiguousarray(words).reshape(g, 128, n, -1)
    if fmt == "e4m3":
        vals = words.view(ml_dtypes.float8_e4m3fn).astype(np.float64)
    else:
        nib = np.empty((g, 128, n, 4), np.uint8)
        nib[..., 0::2] = words & 0xF
        nib[..., 1::2] = words >> 4
        vals = E2M1[nib]
    vals = vals * np.repeat(np.exp2(scales.astype(np.float64) - 127.0), 8, axis=1)[..., None]
    return vals.transpose(0, 1, 3, 2).reshape(g * 512, n)


def gelu(v):
    return 0.5 * v * (1.0 + np.tanh(np.sqrt(2.0 / np.pi) * (v + 0.044715 * v**3)))


K, K2, H, N, T, T2, S, P = 1024, 512, 512, 384, 2048, 2048, 1024, 512

def setup_inputs():
    n = np.random.standard_normal
    s, s2, u = mx_kscale(K)[:, None], mx_kscale(K2)[:, None], mx_kscale(H)[:, None]
    tab_words, tab_scales = pack_weight(n((K, T)) * s, "e4m3")
    tab2_words, tab2_scales = pack_weight(n((K2, T)) * s2, "e4m3")
    w2_words, w2_scales = pack_weight(0.6 * n((K2, H)) / np.sqrt(K2) / s2, "e4m3")
    w4_words, w4_scales = pack_weight(0.7 * n((K, N)) / np.sqrt(K) / s, "e2m1")
    perm = np.random.permutation(T2)
    return {
        "tab_words": tab_words, "tab_scales": tab_scales,
        "tab2_words": tab2_words, "tab2_scales": tab2_scales,
        "offs": striped(np.random.permutation(T)[:S]),
        "offs2": striped(np.random.permutation(T)[:P]),
        "pos1": striped(np.random.permutation(S)[:P]),
        "offs3": striped(perm[:S]), "offs4": striped(perm[S:S + P]),
        "w1": (0.5 * n((K, H)) / np.sqrt(K) / s).astype(np.float32),
        "w2_words": w2_words, "w2_scales": w2_scales,
        "w3": (1.2 * n((H, N)) / np.sqrt(H) / u).astype(np.float32),
        "w4_words": w4_words, "w4_scales": w4_scales,
        "w5": (1.2 * n((H, N)) / np.sqrt(H) / u).astype(np.float32),
        "g1": (2.0 * np.exp(0.3 * n(H)) * u[:, 0]).astype(np.float32),
        "g2": (np.exp(0.3 * n(H)) * u[:, 0]).astype(np.float32),
        "page1": n((N, T2)).astype(np.float32),
        "wg1": np.exp(0.3 * n((128, S))).astype(np.float32),
        "wg2": np.exp(0.3 * n((128, P))).astype(np.float32)}

def reference(tab_words, tab_scales, tab2_words, tab2_scales, offs, offs2, pos1, offs3, offs4, w1, w2_words, w2_scales, w3, w4_words, w4_scales, w5, g1, g2, page1, wg1, wg2):
    v = unpack_weight(tab_words, tab_scales, "e4m3")[:, unstriped(offs)]
    v2 = unpack_weight(tab2_words, tab2_scales, "e4m3")[:, unstriped(offs2)]
    h1 = mxq(f64(w1), 0, "e4m3").T @ v
    h2 = unpack_weight(w2_words, w2_scales, "e4m3").T @ v2
    z1 = f64(g1)[:, None] * np.sin(h1)
    z2 = f64(g2)[:, None] * np.abs(h2 - h1[:, unstriped(pos1)])
    y1 = mxq(f64(w3), 0, "e4m3").T @ mxq(z1, 0, "e4m3") + unpack_weight(w4_words, w4_scales, "e2m1").T @ v
    y2 = mxq(f64(w5), 0, "e4m3").T @ mxq(z2, 0, "e4m3")
    out = f64(page1).copy()
    out[:, unstriped(offs3)] = np.tile(f64(wg1), (N // 128, 1)) * y1
    out[:, unstriped(offs4)] = np.tile(f64(wg2), (N // 128, 1)) * y2
    return out

@@ -1,0 +1,296 @@
+from contextlib import ExitStack
+
+import concourse.mybir as mybir
+
+K, K2, H, N, T, S, PN = 1024, 512, 512, 384, 2048, 1024, 512
+FLOPS = 2751463424
+
+F32 = mybir.dt.float32
+BF16 = mybir.dt.bfloat16
+I32 = mybir.dt.int32
+U32 = mybir.dt.uint32
+U16 = mybir.dt.uint16
+U8 = mybir.dt.uint8
+E4M3 = mybir.dt.float8_e4m3fn_x4
+E2M1 = mybir.dt.float4_e2m1fn_x4
+ACT = mybir.ActivationFunctionType
+ALU = mybir.AluOpType
+
+P = 128
+CH = 256
+NCH = S // CH
+NT = N // P
+
+
+def tile_list_tariff_check_slots_kernel(
+    tc, tab_words, tab_scales, tab2_words, tab2_scales, offs, offs2, pos1, offs3, offs4,
+    w1, w2_words, w2_scales, w3, w4_words, w4_scales, w5, g1, g2, page1, wg1, wg2, out,
+):
+    nc = tc.nc
+    with ExitStack() as ctx:
+        keep = ctx.enter_context(tc.tile_pool(name="keep", bufs=1))
+        work = ctx.enter_context(tc.tile_pool(name="work", bufs=2))
+        stage = ctx.enter_context(tc.tile_pool(name="stage", bufs=4))
+        psum = ctx.enter_context(tc.psum_pool(name="psum", bufs=4))
+
+        def kt(name, shape, dtype):
+            return keep.tile(shape, dtype, name=name, align_bytes=64)
+
+        def load_list(name, src):
+            tile = keep.tile(list(src.shape), U16, name=name)
+            nc.sync.dma_start(tile[:], src)
+            return tile
+
+        def load_scale_rows(queue, tile, src):
+            passes = src.shape[0]
+            for q in range(4):
+                queue.dma_start(
+                    tile[32 * q : 32 * q + 4, :].bitcast(I32).rearrange("r (a c) -> r a c", a=passes),
+                    src[:, 4 * q : 4 * q + 4, :].rearrange("a r c -> r a c").bitcast(I32),
+                )
+
+        def load_words(tile, src):
+            nc.sync.dma_start(tile[:].bitcast(I32), src.rearrange("p c i -> p (c i)").bitcast(I32))
+
+        def load_rows(tile, rows):
+            nc.sync.dma_start(tile[:], rows.rearrange("(p j) c -> p j c", j=4))
+
+        def quantise(codes, scales, grouped):
+            nc.vector.quantize_mx(out=codes.bitcast(E4M3), scales=scales, in_=grouped)
+
+        def woven(ap):
+            return ap.rearrange("p (c i t) -> p c t i", i=4, t=4)
+
+        def planes(ap):
+            return ap.rearrange("p t (c i) -> p c t i", i=4)
+
+        tab_s = kt("tab_s", [P, 2 * T], U8)
+        nc.vector.memset(tab_s[:].bitcast(I32), 0)
+        l_offs = load_list("l_offs", offs)
+        tab_w = [kt("tab_w%d" % a, [P, T], U32) for a in range(2)]
+        w1_raw = [kt("w1_raw%d" % a, [P, 4, H], F32) for a in range(2)]
+        load_words(tab_w[0], tab_words[0])
+        load_scale_rows(nc.sync, tab_s, tab_scales)
+        for a in range(2):
+            load_rows(w1_raw[a], w1[512 * a : 512 * (a + 1), :])
+        load_words(tab_w[1], tab_words[1])
+        g1_sb = kt("g1_sb", [P, 4], F32)
+        nc.sync.dma_start(g1_sb[:], g1.rearrange("(p t) -> p t", t=4))
+
+        tab2_s = kt("tab2_s", [P, T], U8)
+        w4_s = kt("w4_s", [P, 2 * N], U8)
+        w2_s_raw = kt("w2_s_raw", [P, H], U8)
+        for tile in (tab2_s, w4_s, w2_s_raw):
+            nc.gpsimd.memset(tile[:].bitcast(I32), 0)
+        g2_sb = kt("g2_sb", [P, 4], F32)
+        load_scale_rows(nc.gpsimd, tab2_s, tab2_scales)
+        load_scale_rows(nc.gpsimd, w4_s, w4_scales)
+        load_scale_rows(nc.gpsimd, w2_s_raw, w2_scales)
+        nc.gpsimd.dma_start(g2_sb[:], g2.rearrange("(p t) -> p t", t=4))
+
+        tab2_w = kt("tab2_w", [P, T], U32)
+        l_offs2 = load_list("l_offs2", offs2)
+        load_words(tab2_w, tab2_words[0])
+        w3_raw = kt("w3_raw", [P, 4, N], F32)
+        load_rows(w3_raw, w3)
+        w4_w = kt("w4_w", [P, 2, 2 * N], U8)
+        nc.sync.dma_start(w4_w[:].bitcast(I32), w4_words.rearrange("a p c -> p a c").bitcast(I32))
+        l_offs3 = load_list("l_offs3", offs3)
+        wg1_sb = kt("wg1_sb", [P, S], F32)
+        nc.sync.dma_start(wg1_sb[:], wg1)
+        page = [kt("page%d" % n, [P, T], F32) for n in range(NT)]
+        for n in range(NT):
+            nc.sync.dma_start(page[n][:], page1[P * n : P * (n + 1), :])
+        w2_w_raw = kt("w2_w_raw", [P, H], U32)
+        load_words(w2_w_raw, w2_words[0])
+        l_pos1 = load_list("l_pos1", pos1)
+        w5_raw = kt("w5_raw", [P, 4, N], F32)
+        load_rows(w5_raw, w5)
+        l_offs4 = load_list("l_offs4", offs4)
+        wg2_sb = kt("wg2_sb", [P, PN], F32)
+        nc.sync.dma_start(wg2_sb[:], wg2)
+
+        v_s = [kt("v_s%d" % a, [P, S], U8) for a in range(2)]
+        v_w0 = kt("v_w0", [P, S], U32)
+        v_w1 = [kt("v_w1_%d" % c, [P, CH], U32) for c in range(NCH)]
+        nc.vector.tensor_copy(v_w0[:], tab_w[0][:].indirect(l_offs[:]))
+        for a in range(2):
+            nc.vector.tensor_copy(v_s[a][:], tab_s[:, T * a : T * (a + 1)].indirect(l_offs[:]))
+
+        w1_c = [kt("w1_c%d" % a, [P, H], U32) for a in range(2)]
+        w1_s = [kt("w1_s%d" % a, [P, H], U8) for a in range(2)]
+        for a in range(2):
+            w1_g = work.tile([P, 4 * H], BF16, name="w1_g", align_bytes=64)
+            nc.scalar.copy(
+                w1_g[:].rearrange("p (t m j) -> p m j t", t=4, j=4),
+                w1_raw[a][:].rearrange("p j (m t) -> p m j t", t=4),
+            )
+            quantise(w1_c[a][:], w1_s[a][:], w1_g[:])
+
+        def list_cols(tile, c):
+            return tile[:, (CH // 16) * c : (CH // 16) * (c + 1)]
+
+        for c in range(NCH):
+            nc.vector.tensor_copy(v_w1[c][:], tab_w[1][:].indirect(list_cols(l_offs, c)))
+
+        g_m4 = kt("g_m4", [P, 4], F32)
+        g_3 = kt("g_3", [P, 4], F32)
+        nc.vector.tensor_scalar(g_m4[:], g1_sb[:], -4.0, None, ALU.mult)
+        nc.vector.tensor_scalar(g_3[:], g1_sb[:], 3.0, None, ALU.mult)
+
+        w3_g = kt("w3_g", [P, 4 * N], BF16)
+        w3_c = kt("w3_c", [P, N], U32)
+        w3_s = kt("w3_s", [P, N], U8)
+        v2_w = kt("v2_w", [P, PN], U32)
+        v2_s = kt("v2_s", [P, PN], U8)
+        nc.vector.tensor_copy(v2_s[:], tab2_s[:].indirect(l_offs2[:]))
+        nc.vector.tensor_copy(v2_w[:], tab2_w[:].indirect(l_offs2[:]))
+        nc.vector.tensor_copy(woven(w3_g[:]), planes(w3_raw[:]))
+        quantise(w3_c[:], w3_s[:], w3_g[:])
+
+        w2_c = kt("w2_c", [P, H], U32)
+        w2_s = kt("w2_s", [P, H], U8)
+        nc.gpsimd.tensor_copy(
+            w2_s[:].rearrange("p (t m) -> p t m", t=4), w2_s_raw[:].rearrange("p (m t) -> p t m", t=4)
+        )
+        nc.gpsimd.tensor_copy(
+            w2_c[:].rearrange("p (t m) -> p t m", t=4), w2_w_raw[:].rearrange("p (m t) -> p t m", t=4)
+        )
+
+        h1 = [kt("h1_%d" % t, [P, S], F32) for t in range(4)]
+        h2 = kt("h2", [P, 4, PN], F32)
+
+        def v_operand(a, c):
+            cols = slice(CH * c, CH * (c + 1))
+            words = v_w0[:, cols] if a == 0 else v_w1[c][:]
+            return words.bitcast(E4M3), v_s[a][:, cols]
+
+        def stage1(c):
+            banks = []
+            for b in range(2):
+                bank = psum.tile([P, 2, CH], F32, name="h_bank")
+                for a in range(2):
+                    words, scales = v_operand(a, c)
+                    for i in range(2):
+                        cols = slice(P * (2 * b + i), P * (2 * b + i + 1))
+                        nc.tensor.matmul_mx(
+                            out=bank[:, i, :], lhsT=w1_c[a][:, cols].bitcast(E4M3), lhsT_scale=w1_s[a][:, cols],
+                            rhs=words, rhs_scale=scales, start=(a == 0 and i == 0), stop=(a == 1 and i == 1),
+                        )
+                banks.append(bank)
+            return banks
+
+        def sines(banks):
+            s = work.tile([P, 4, CH], F32, name="s")
+            for b in range(2):
+                nc.scalar.activation(s[:, 2 * b : 2 * b + 2, :], banks[b][:], ACT.Sin, scale=1.0 / 3.0)
+            return s
+
+        def factors(s):
+            u = work.tile([P, 4, CH], F32, name="u")
+            nc.scalar.activation(u[:], s[:], ACT.Square)
+            for t in range(4):
+                nc.scalar.activation(
+                    u[:, t, :], u[:, t, :], ACT.Identity, scale=g_m4[:, t : t + 1], bias=g_3[:, t : t + 1]
+                )
+            return u
+
+        def keep_h1(banks, c):
+            for t in range(4):
+                nc.scalar.copy(h1[t][:, CH * c : CH * (c + 1)], banks[t // 2][:, t % 2, :])
+
+        def quantise_z1(s, u):
+            z_g = work.tile([P, 4 * CH], BF16, name="z_g", align_bytes=64)
+            z_c = work.tile([P, CH], U32, name="z_c", align_bytes=64)
+            z_s = work.tile([P, CH], U8, name="z_s", align_bytes=64)
+            nc.vector.tensor_tensor(woven(z_g[:]), planes(u[:]), planes(s[:]), ALU.mult)
+            quantise(z_c[:], z_s[:], z_g[:])
+            return z_c, z_s
+
+        def stage2(c, z):
+            z_c, z_s = z
+            banks = []
+            for n in range(NT):
+                bank = psum.tile([P, 2 * CH], F32, name="y_bank")
+                for a in range(2):
+                    words, scales = v_operand(a, c)
+                    nc.tensor.matmul_mx(
+                        out=bank[:, :CH], lhsT=w4_w[:, a, 2 * P * n : 2 * P * (n + 1)].bitcast(E2M1),
+                        lhsT_scale=w4_s[:, N * a + P * n : N * a + P * (n + 1)],
+                        rhs=words, rhs_scale=scales, start=(a == 0), stop=False,
+                    )
+                cols = slice(P * n, P * (n + 1))
+                nc.tensor.matmul_mx(
+                    out=bank[:, :CH], lhsT=w3_c[:, cols].bitcast(E4M3), lhsT_scale=w3_s[:, cols],
+                    rhs=z_c[:].bitcast(E4M3), rhs_scale=z_s[:], start=False, stop=True,
+                )
+                banks.append(bank)
+            return banks
+
+        def place1(c, n, bank):
+            y = stage.tile([P, CH], F32, name="y")
+            nc.scalar.copy(y[:], bank[:, :CH])
+            nc.vector.tensor_tensor(
+                page[n][:].indirect(list_cols(l_offs3, c)), y[:], wg1_sb[:, CH * c : CH * (c + 1)], ALU.mult
+            )
+
+        h_banks = stage1(0)
+        s = sines(h_banks)
+        z = quantise_z1(s, factors(s))
+        keep_h1(h_banks, 0)
+        y_banks = stage2(0, z)
+        for c in range(1, NCH):
+            h_banks = stage1(c)
+            s = sines(h_banks)
+            place1(c - 1, 0, y_banks[0])
+            place1(c - 1, 1, y_banks[1])
+            z = quantise_z1(s, factors(s))
+            if c < NCH - 1:
+                place1(c - 1, 2, y_banks[2])
+            held = y_banks[2]
+            keep_h1(h_banks, c)
+            y_banks = stage2(c, z)
+
+        d = kt("d", [P, 4, PN], F32)
+        for t in range(4):
+            bank = psum.tile([P, 2, CH], F32, name="h_bank")
+            cols = slice(P * t, P * (t + 1))
+            flat = bank[:].rearrange("p i c -> p (i c)")
+            nc.tensor.matmul_mx(
+                out=flat, lhsT=w2_c[:, cols].bitcast(E4M3), lhsT_scale=w2_s[:, cols],
+                rhs=v2_w[:].bitcast(E4M3), rhs_scale=v2_s[:], start=True, stop=True,
+            )
+            nc.scalar.copy(h2[:, t, :], flat)
+            nc.vector.tensor_tensor(d[:, t, :], h1[t][:].indirect(l_pos1[:]), h2[:, t, :], ALU.subtract)
+        place1(NCH - 2, 2, held)
+        place1(NCH - 1, 0, y_banks[0])
+        place1(NCH - 1, 1, y_banks[1])
+
+        w5_g = kt("w5_g", [P, 4 * N], BF16)
+        w5_c = kt("w5_c", [P, N], U32)
+        w5_s = kt("w5_s", [P, N], U8)
+        nc.scalar.copy(woven(w5_g[:]), planes(w5_raw[:]))
+        quantise(w5_c[:], w5_s[:], w5_g[:])
+
+        z2_p = kt("z2_p", [P, 4, PN], BF16)
+        for t in range(4):
+            nc.scalar.activation(d[:, t, :], d[:, t, :], ACT.Abs)
+            nc.scalar.activation(z2_p[:, t, :], d[:, t, :], ACT.Copy, scale=g2_sb[:, t : t + 1])
+        z2_g = kt("z2_g", [P, 4 * PN], BF16)
+        z2_c = kt("z2_c", [P, PN], U32)
+        z2_s = kt("z2_s", [P, PN], U8)
+        nc.scalar.copy(woven(z2_g[:]), planes(z2_p[:]))
+        quantise(z2_c[:], z2_s[:], z2_g[:])
+        place1(NCH - 1, 2, y_banks[2])
+
+        for n in range(NT):
+            bank = psum.tile([P, 2 * CH], F32, name="y_bank")
+            cols = slice(P * n, P * (n + 1))
+            nc.tensor.matmul_mx(
+                out=bank[:], lhsT=w5_c[:, cols].bitcast(E4M3), lhsT_scale=w5_s[:, cols],
+                rhs=z2_c[:].bitcast(E4M3), rhs_scale=z2_s[:], start=True, stop=True,
+            )
+            y2 = work.tile([P, PN], F32, name="y2")
+            nc.scalar.copy(y2[:], bank[:])
+            nc.vector.tensor_tensor(page[n][:].indirect(l_offs4[:]), y2[:], wg2_sb[:], ALU.mult)
+            nc.sync.dma_start(out[P * n : P * (n + 1), :], page[n][:])

@@ -64,43 +64,50 @@ def tile_list_tariff_check_slots_kernel(
         def planes(ap):
             return ap.rearrange("p t (c i) -> p c t i", i=4)
 
-        tab_s = kt("tab_s", [P, 2 * T], U8)
+        tab_s = kt("tab_s", [P, T], U8)
         nc.vector.memset(tab_s[:].bitcast(I32), 0)
-        l_offs = load_list("l_offs", offs)
-        tab_w = [kt("tab_w%d" % a, [P, T], U32) for a in range(2)]
-        w1_raw = [kt("w1_raw%d" % a, [P, 4, H], F32) for a in range(2)]
-        load_words(tab_w[0], tab_words[0])
-        load_scale_rows(nc.sync, tab_s, tab_scales)
-        for a in range(2):
-            load_rows(w1_raw[a], w1[512 * a : 512 * (a + 1), :])
-        load_words(tab_w[1], tab_words[1])
-        g1_sb = kt("g1_sb", [P, 4], F32)
-        nc.sync.dma_start(g1_sb[:], g1.rearrange("(p t) -> p t", t=4))
-
         tab2_s = kt("tab2_s", [P, T], U8)
         w4_s = kt("w4_s", [P, 2 * N], U8)
         w2_s_raw = kt("w2_s_raw", [P, H], U8)
-        for tile in (tab2_s, w4_s, w2_s_raw):
+        v_s = [kt("v_s%d" % a, [P, S], U8) for a in range(2)]
+        for tile in (v_s[1], w4_s, tab2_s, w2_s_raw):
             nc.gpsimd.memset(tile[:].bitcast(I32), 0)
+
+        g1_sb = kt("g1_sb", [P, 4], F32)
         g2_sb = kt("g2_sb", [P, 4], F32)
-        load_scale_rows(nc.gpsimd, tab2_s, tab2_scales)
         load_scale_rows(nc.gpsimd, w4_s, w4_scales)
+        load_scale_rows(nc.gpsimd, tab2_s, tab2_scales)
         load_scale_rows(nc.gpsimd, w2_s_raw, w2_scales)
         nc.gpsimd.dma_start(g2_sb[:], g2.rearrange("(p t) -> p t", t=4))
 
-        tab2_w = kt("tab2_w", [P, T], U32)
-        l_offs2 = load_list("l_offs2", offs2)
-        load_words(tab2_w, tab2_words[0])
+        l_offs = load_list("l_offs", offs)
+        l_offs3 = load_list("l_offs3", offs3)
+        nc.sync.dma_start(g1_sb[:], g1.rearrange("(p t) -> p t", t=4))
+        tab_w = [kt("tab_w%d" % a, [P, T], U32) for a in range(2)]
+        w1_raw = [kt("w1_raw%d" % a, [P, 4, H], F32) for a in range(2)]
+        load_rows(w1_raw[0], w1[:512, :])
+        for q in range(4):
+            nc.sync.dma_start(
+                tab_s[32 * q : 32 * q + 8, :].bitcast(I32), tab_scales[:, 4 * q : 4 * q + 4, :].bitcast(I32)
+            )
+        load_rows(w1_raw[1], w1[512:, :])
+        for a in range(2):
+            load_words(tab_w[a], tab_words[a])
         w3_raw = kt("w3_raw", [P, 4, N], F32)
         load_rows(w3_raw, w3)
         w4_w = kt("w4_w", [P, 2, 2 * N], U8)
         nc.sync.dma_start(w4_w[:].bitcast(I32), w4_words.rearrange("a p c -> p a c").bitcast(I32))
-        l_offs3 = load_list("l_offs3", offs3)
-        wg1_sb = kt("wg1_sb", [P, S], F32)
-        nc.sync.dma_start(wg1_sb[:], wg1)
+        wg1_first = kt("wg1_first", [P, CH], F32)
+        nc.sync.dma_start(wg1_first[:], wg1[:, :CH])
         page = [kt("page%d" % n, [P, T], F32) for n in range(NT)]
-        for n in range(NT):
+        for n in range(2):
             nc.sync.dma_start(page[n][:], page1[P * n : P * (n + 1), :])
+        l_offs2 = load_list("l_offs2", offs2)
+        tab2_w = kt("tab2_w", [P, T], U32)
+        load_words(tab2_w, tab2_words[0])
+        nc.sync.dma_start(page[2][:], page1[2 * P :, :])
+        wg1_rest = kt("wg1_rest", [P, S - CH], F32)
+        nc.sync.dma_start(wg1_rest[:], wg1[:, CH:])
         w2_w_raw = kt("w2_w_raw", [P, H], U32)
         load_words(w2_w_raw, w2_words[0])
         l_pos1 = load_list("l_pos1", pos1)
@@ -110,12 +117,8 @@ def tile_list_tariff_check_slots_kernel(
         wg2_sb = kt("wg2_sb", [P, PN], F32)
         nc.sync.dma_start(wg2_sb[:], wg2)
 
-        v_s = [kt("v_s%d" % a, [P, S], U8) for a in range(2)]
-        v_w0 = kt("v_w0", [P, S], U32)
-        v_w1 = [kt("v_w1_%d" % c, [P, CH], U32) for c in range(NCH)]
-        nc.vector.tensor_copy(v_w0[:], tab_w[0][:].indirect(l_offs[:]))
-        for a in range(2):
-            nc.vector.tensor_copy(v_s[a][:], tab_s[:, T * a : T * (a + 1)].indirect(l_offs[:]))
+        v_w = [[kt("v_w%d_%d" % (a, c), [P, CH], U32) for c in range(NCH)] for a in range(2)]
+        nc.vector.tensor_copy(v_s[0][:], tab_s[:].indirect(l_offs[:]))
 
         w1_c = [kt("w1_c%d" % a, [P, H], U32) for a in range(2)]
         w1_s = [kt("w1_s%d" % a, [P, H], U8) for a in range(2)]
@@ -127,11 +130,17 @@ def tile_list_tariff_check_slots_kernel(
             )
             quantise(w1_c[a][:], w1_s[a][:], w1_g[:])
 
+        for q in range(4):
+            nc.scalar.dma_start(
+                v_s[1][32 * q : 32 * q + 4, :].bitcast(I32), v_s[0][32 * q + 4 : 32 * q + 8, :].bitcast(I32)
+            )
+
         def list_cols(tile, c):
             return tile[:, (CH // 16) * c : (CH // 16) * (c + 1)]
 
         for c in range(NCH):
-            nc.vector.tensor_copy(v_w1[c][:], tab_w[1][:].indirect(list_cols(l_offs, c)))
+            for a in range(2):
+                nc.vector.tensor_copy(v_w[a][c][:], tab_w[a][:].indirect(list_cols(l_offs, c)))
 
         g_m4 = kt("g_m4", [P, 4], F32)
         g_3 = kt("g_3", [P, 4], F32)
@@ -143,10 +152,10 @@ def tile_list_tariff_check_slots_kernel(
         w3_s = kt("w3_s", [P, N], U8)
         v2_w = kt("v2_w", [P, PN], U32)
         v2_s = kt("v2_s", [P, PN], U8)
-        nc.vector.tensor_copy(v2_s[:], tab2_s[:].indirect(l_offs2[:]))
-        nc.vector.tensor_copy(v2_w[:], tab2_w[:].indirect(l_offs2[:]))
         nc.vector.tensor_copy(woven(w3_g[:]), planes(w3_raw[:]))
         quantise(w3_c[:], w3_s[:], w3_g[:])
+        nc.vector.tensor_copy(v2_s[:], tab2_s[:].indirect(l_offs2[:]))
+        nc.vector.tensor_copy(v2_w[:], tab2_w[:].indirect(l_offs2[:]))
 
         w2_c = kt("w2_c", [P, H], U32)
         w2_s = kt("w2_s", [P, H], U8)
@@ -162,15 +171,15 @@ def tile_list_tariff_check_slots_kernel(
 
         def v_operand(a, c):
             cols = slice(CH * c, CH * (c + 1))
-            words = v_w0[:, cols] if a == 0 else v_w1[c][:]
-            return words.bitcast(E4M3), v_s[a][:, cols]
+            return v_w[a][c][:].bitcast(E4M3), v_s[a][:, cols]
 
         def stage1(c):
             banks = []
             for b in range(2):
                 bank = psum.tile([P, 2, CH], F32, name="h_bank")
                 for a in range(2):
-                    words, scales = v_operand(a, c)
+                    words = v_w[a][c][:].bitcast(E4M3)
+                    scales = v_s[0][4 * a :, CH * c : CH * (c + 1)]
                     for i in range(2):
                         cols = slice(P * (2 * b + i), P * (2 * b + i + 1))
                         nc.tensor.matmul_mx(
@@ -229,42 +238,52 @@ def tile_list_tariff_check_slots_kernel(
 
         def place1(c, n, bank):
             y = stage.tile([P, CH], F32, name="y")
-            nc.scalar.copy(y[:], bank[:, :CH])
-            nc.vector.tensor_tensor(
-                page[n][:].indirect(list_cols(l_offs3, c)), y[:], wg1_sb[:, CH * c : CH * (c + 1)], ALU.mult
-            )
+            if (c, n) == (0, 0):
+                nc.vector.tensor_copy(y[:], bank[:, :CH])
+            else:
+                nc.scalar.copy(y[:], bank[:, :CH])
+            gains = wg1_first[:] if c == 0 else wg1_rest[:, CH * (c - 1) : CH * c]
+            nc.vector.tensor_tensor(page[n][:].indirect(list_cols(l_offs3, c)), y[:], gains, ALU.mult)
 
+        def stage1_declarations():
+            for t in range(4):
+                bank = psum.tile([P, 2, CH], F32, name="h_bank")
+                cols = slice(P * t, P * (t + 1))
+                flat = bank[:].rearrange("p i c -> p (i c)")
+                nc.tensor.matmul_mx(
+                    out=flat, lhsT=w2_c[:, cols].bitcast(E4M3), lhsT_scale=w2_s[:, cols],
+                    rhs=v2_w[:].bitcast(E4M3), rhs_scale=v2_s[:], start=True, stop=True,
+                )
+                nc.scalar.copy(h2[:, t, :], flat)
+
+        last = NCH - 1
         h_banks = stage1(0)
         s = sines(h_banks)
         z = quantise_z1(s, factors(s))
         keep_h1(h_banks, 0)
         y_banks = stage2(0, z)
-        for c in range(1, NCH):
+        for c in range(1, last):
             h_banks = stage1(c)
             s = sines(h_banks)
             place1(c - 1, 0, y_banks[0])
             place1(c - 1, 1, y_banks[1])
             z = quantise_z1(s, factors(s))
-            if c < NCH - 1:
-                place1(c - 1, 2, y_banks[2])
-            held = y_banks[2]
+            place1(c - 1, 2, y_banks[2])
             keep_h1(h_banks, c)
             y_banks = stage2(c, z)
 
+        place1(last - 1, 0, y_banks[0])
+        place1(last - 1, 1, y_banks[1])
+        stage1_declarations()
+        h_banks = stage1(last)
+        s = sines(h_banks)
+        keep_h1(h_banks, last)
         d = kt("d", [P, 4, PN], F32)
         for t in range(4):
-            bank = psum.tile([P, 2, CH], F32, name="h_bank")
-            cols = slice(P * t, P * (t + 1))
-            flat = bank[:].rearrange("p i c -> p (i c)")
-            nc.tensor.matmul_mx(
-                out=flat, lhsT=w2_c[:, cols].bitcast(E4M3), lhsT_scale=w2_s[:, cols],
-                rhs=v2_w[:].bitcast(E4M3), rhs_scale=v2_s[:], start=True, stop=True,
-            )
-            nc.scalar.copy(h2[:, t, :], flat)
             nc.vector.tensor_tensor(d[:, t, :], h1[t][:].indirect(l_pos1[:]), h2[:, t, :], ALU.subtract)
-        place1(NCH - 2, 2, held)
-        place1(NCH - 1, 0, y_banks[0])
-        place1(NCH - 1, 1, y_banks[1])
+        z = quantise_z1(s, factors(s))
+        place1(last - 1, 2, y_banks[2])
+        y_banks = stage2(last, z)
 
         w5_g = kt("w5_g", [P, 4 * N], BF16)
         w5_c = kt("w5_c", [P, N], U32)
@@ -276,6 +295,8 @@ def tile_list_tariff_check_slots_kernel(
         for t in range(4):
             nc.scalar.activation(d[:, t, :], d[:, t, :], ACT.Abs)
             nc.scalar.activation(z2_p[:, t, :], d[:, t, :], ACT.Copy, scale=g2_sb[:, t : t + 1])
+        place1(last, 0, y_banks[0])
+        place1(last, 1, y_banks[1])
         z2_g = kt("z2_g", [P, 4 * PN], BF16)
         z2_c = kt("z2_c", [P, PN], U32)
         z2_s = kt("z2_s", [P, PN], U8)

@@ -105,11 +105,11 @@ def tile_list_tariff_check_slots_kernel(
         l_offs2 = load_list("l_offs2", offs2)
         tab2_w = kt("tab2_w", [P, T], U32)
         load_words(tab2_w, tab2_words[0])
+        w2_w_raw = kt("w2_w_raw", [P, H], U32)
+        load_words(w2_w_raw, w2_words[0])
         nc.sync.dma_start(page[2][:], page1[2 * P :, :])
         wg1_rest = kt("wg1_rest", [P, S - CH], F32)
         nc.sync.dma_start(wg1_rest[:], wg1[:, CH:])
-        w2_w_raw = kt("w2_w_raw", [P, H], U32)
-        load_words(w2_w_raw, w2_words[0])
         l_pos1 = load_list("l_pos1", pos1)
         w5_raw = kt("w5_raw", [P, 4, N], F32)
         load_rows(w5_raw, w5)
@@ -158,11 +158,7 @@ def tile_list_tariff_check_slots_kernel(
         nc.vector.tensor_copy(v2_w[:], tab2_w[:].indirect(l_offs2[:]))
 
         w2_c = kt("w2_c", [P, H], U32)
-        w2_s = kt("w2_s", [P, H], U8)
-        nc.gpsimd.tensor_copy(
-            w2_s[:].rearrange("p (t m) -> p t m", t=4), w2_s_raw[:].rearrange("p (m t) -> p t m", t=4)
-        )
-        nc.gpsimd.tensor_copy(
+        nc.scalar.copy(
             w2_c[:].rearrange("p (t m) -> p t m", t=4), w2_w_raw[:].rearrange("p (m t) -> p t m", t=4)
         )
 
@@ -245,7 +241,7 @@ def tile_list_tariff_check_slots_kernel(
             gains = wg1_first[:] if c == 0 else wg1_rest[:, CH * (c - 1) : CH * c]
             nc.vector.tensor_tensor(page[n][:].indirect(list_cols(l_offs3, c)), y[:], gains, ALU.mult)
 
-        def stage1_declarations():
+        def stage1_declarations(w2_s):
             for t in range(4):
                 bank = psum.tile([P, 2, CH], F32, name="h_bank")
                 cols = slice(P * t, P * (t + 1))
@@ -268,13 +264,18 @@ def tile_list_tariff_check_slots_kernel(
             place1(c - 1, 0, y_banks[0])
             place1(c - 1, 1, y_banks[1])
             z = quantise_z1(s, factors(s))
+            if c == 1:
+                w2_s = work.tile([P, H], U8, name="z_g", align_bytes=64)
+                nc.vector.tensor_copy(
+                    w2_s[:].rearrange("p (t m) -> p t m", t=4), w2_s_raw[:].rearrange("p (m t) -> p t m", t=4)
+                )
             place1(c - 1, 2, y_banks[2])
             keep_h1(h_banks, c)
             y_banks = stage2(c, z)
 
         place1(last - 1, 0, y_banks[0])
         place1(last - 1, 1, y_banks[1])
-        stage1_declarations()
+        stage1_declarations(w2_s)
         h_banks = stage1(last)
         s = sines(h_banks)
         keep_h1(h_banks, last)

from contextlib import ExitStack

import concourse.mybir as mybir

K, K2, H, N, T, S, PN = 1024, 512, 512, 384, 2048, 1024, 512
FLOPS = 2751463424

F32 = mybir.dt.float32
BF16 = mybir.dt.bfloat16
I32 = mybir.dt.int32
U32 = mybir.dt.uint32
U16 = mybir.dt.uint16
U8 = mybir.dt.uint8
E4M3 = mybir.dt.float8_e4m3fn_x4
E2M1 = mybir.dt.float4_e2m1fn_x4
ACT = mybir.ActivationFunctionType
ALU = mybir.AluOpType

P = 128
CH = 256
NCH = S // CH
NT = N // P


def tile_list_tariff_check_slots_kernel(
    tc, tab_words, tab_scales, tab2_words, tab2_scales, offs, offs2, pos1, offs3, offs4,
    w1, w2_words, w2_scales, w3, w4_words, w4_scales, w5, g1, g2, page1, wg1, wg2, out,
):
    nc = tc.nc
    with ExitStack() as ctx:
        keep = ctx.enter_context(tc.tile_pool(name="keep", bufs=1))
        work = ctx.enter_context(tc.tile_pool(name="work", bufs=2))
        stage = ctx.enter_context(tc.tile_pool(name="stage", bufs=4))
        psum = ctx.enter_context(tc.psum_pool(name="psum", bufs=4))

        def kt(name, shape, dtype):
            return keep.tile(shape, dtype, name=name, align_bytes=64)

        def load_list(name, src):
            tile = keep.tile(list(src.shape), U16, name=name)
            nc.sync.dma_start(tile[:], src)
            return tile

        def load_scale_rows(queue, tile, src):
            passes = src.shape[0]
            for q in range(4):
                queue.dma_start(
                    tile[32 * q : 32 * q + 4, :].bitcast(I32).rearrange("r (a c) -> r a c", a=passes),
                    src[:, 4 * q : 4 * q + 4, :].rearrange("a r c -> r a c").bitcast(I32),
                )

        def load_words(tile, src):
            nc.sync.dma_start(tile[:].bitcast(I32), src.rearrange("p c i -> p (c i)").bitcast(I32))

        def load_rows(tile, rows):
            nc.sync.dma_start(tile[:], rows.rearrange("(p j) c -> p j c", j=4))

        def quantise(codes, scales, grouped):
            nc.vector.quantize_mx(out=codes.bitcast(E4M3), scales=scales, in_=grouped)

        def woven(ap):
            return ap.rearrange("p (c i t) -> p c t i", i=4, t=4)

        def planes(ap):
            return ap.rearrange("p t (c i) -> p c t i", i=4)

        tab_s = kt("tab_s", [P, T], U8)
        nc.vector.memset(tab_s[:].bitcast(I32), 0)
        tab2_s = kt("tab2_s", [P, T], U8)
        w4_s = kt("w4_s", [P, 2 * N], U8)
        w2_s_raw = kt("w2_s_raw", [P, H], U8)
        v_s = [kt("v_s%d" % a, [P, S], U8) for a in range(2)]
        for tile in (v_s[1], w4_s, tab2_s, w2_s_raw):
            nc.gpsimd.memset(tile[:].bitcast(I32), 0)

        g1_sb = kt("g1_sb", [P, 4], F32)
        g2_sb = kt("g2_sb", [P, 4], F32)
        load_scale_rows(nc.gpsimd, w4_s, w4_scales)
        load_scale_rows(nc.gpsimd, tab2_s, tab2_scales)
        load_scale_rows(nc.gpsimd, w2_s_raw, w2_scales)
        nc.gpsimd.dma_start(g2_sb[:], g2.rearrange("(p t) -> p t", t=4))

        l_offs = load_list("l_offs", offs)
        l_offs3 = load_list("l_offs3", offs3)
        nc.sync.dma_start(g1_sb[:], g1.rearrange("(p t) -> p t", t=4))
        tab_w = [kt("tab_w%d" % a, [P, T], U32) for a in range(2)]
        w1_raw = [kt("w1_raw%d" % a, [P, 4, H], F32) for a in range(2)]
        load_rows(w1_raw[0], w1[:512, :])
        for q in range(4):
            nc.sync.dma_start(
                tab_s[32 * q : 32 * q + 8, :].bitcast(I32), tab_scales[:, 4 * q : 4 * q + 4, :].bitcast(I32)
            )
        load_rows(w1_raw[1], w1[512:, :])
        for a in range(2):
            load_words(tab_w[a], tab_words[a])
        w3_raw = kt("w3_raw", [P, 4, N], F32)
        load_rows(w3_raw, w3)
        w4_w = kt("w4_w", [P, 2, 2 * N], U8)
        nc.sync.dma_start(w4_w[:].bitcast(I32), w4_words.rearrange("a p c -> p a c").bitcast(I32))
        wg1_first = kt("wg1_first", [P, CH], F32)
        nc.sync.dma_start(wg1_first[:], wg1[:, :CH])
        page = [kt("page%d" % n, [P, T], F32) for n in range(NT)]
        for n in range(2):
            nc.sync.dma_start(page[n][:], page1[P * n : P * (n + 1), :])
        l_offs2 = load_list("l_offs2", offs2)
        tab2_w = kt("tab2_w", [P, T], U32)
        load_words(tab2_w, tab2_words[0])
        w2_w_raw = kt("w2_w_raw", [P, H], U32)
        load_words(w2_w_raw, w2_words[0])
        nc.sync.dma_start(page[2][:], page1[2 * P :, :])
        wg1_rest = kt("wg1_rest", [P, S - CH], F32)
        nc.sync.dma_start(wg1_rest[:], wg1[:, CH:])
        l_pos1 = load_list("l_pos1", pos1)
        w5_raw = kt("w5_raw", [P, 4, N], F32)
        load_rows(w5_raw, w5)
        l_offs4 = load_list("l_offs4", offs4)
        wg2_sb = kt("wg2_sb", [P, PN], F32)
        nc.sync.dma_start(wg2_sb[:], wg2)

        v_w = [[kt("v_w%d_%d" % (a, c), [P, CH], U32) for c in range(NCH)] for a in range(2)]
        nc.vector.tensor_copy(v_s[0][:], tab_s[:].indirect(l_offs[:]))

        w1_c = [kt("w1_c%d" % a, [P, H], U32) for a in range(2)]
        w1_s = [kt("w1_s%d" % a, [P, H], U8) for a in range(2)]
        for a in range(2):
            w1_g = work.tile([P, 4 * H], BF16, name="w1_g", align_bytes=64)
            nc.scalar.copy(
                w1_g[:].rearrange("p (t m j) -> p m j t", t=4, j=4),
                w1_raw[a][:].rearrange("p j (m t) -> p m j t", t=4),
            )
            quantise(w1_c[a][:], w1_s[a][:], w1_g[:])

        for q in range(4):
            nc.scalar.dma_start(
                v_s[1][32 * q : 32 * q + 4, :].bitcast(I32), v_s[0][32 * q + 4 : 32 * q + 8, :].bitcast(I32)
            )

        def list_cols(tile, c):
            return tile[:, (CH // 16) * c : (CH // 16) * (c + 1)]

        for c in range(NCH):
            for a in range(2):
                nc.vector.tensor_copy(v_w[a][c][:], tab_w[a][:].indirect(list_cols(l_offs, c)))

        g_m4 = kt("g_m4", [P, 4], F32)
        g_3 = kt("g_3", [P, 4], F32)
        nc.vector.tensor_scalar(g_m4[:], g1_sb[:], -4.0, None, ALU.mult)
        nc.vector.tensor_scalar(g_3[:], g1_sb[:], 3.0, None, ALU.mult)

        w3_g = kt("w3_g", [P, 4 * N], BF16)
        w3_c = kt("w3_c", [P, N], U32)
        w3_s = kt("w3_s", [P, N], U8)
        v2_w = kt("v2_w", [P, PN], U32)
        v2_s = kt("v2_s", [P, PN], U8)
        nc.vector.tensor_copy(woven(w3_g[:]), planes(w3_raw[:]))
        quantise(w3_c[:], w3_s[:], w3_g[:])
        nc.vector.tensor_copy(v2_s[:], tab2_s[:].indirect(l_offs2[:]))
        nc.vector.tensor_copy(v2_w[:], tab2_w[:].indirect(l_offs2[:]))

        w2_c = kt("w2_c", [P, H], U32)
        nc.scalar.copy(
            w2_c[:].rearrange("p (t m) -> p t m", t=4), w2_w_raw[:].rearrange("p (m t) -> p t m", t=4)
        )

        h1 = [kt("h1_%d" % t, [P, S], F32) for t in range(4)]
        h2 = kt("h2", [P, 4, PN], F32)

        def v_operand(a, c):
            cols = slice(CH * c, CH * (c + 1))
            return v_w[a][c][:].bitcast(E4M3), v_s[a][:, cols]

        def stage1(c):
            banks = []
            for b in range(2):
                bank = psum.tile([P, 2, CH], F32, name="h_bank")
                for a in range(2):
                    words = v_w[a][c][:].bitcast(E4M3)
                    scales = v_s[0][4 * a :, CH * c : CH * (c + 1)]
                    for i in range(2):
                        cols = slice(P * (2 * b + i), P * (2 * b + i + 1))
                        nc.tensor.matmul_mx(
                            out=bank[:, i, :], lhsT=w1_c[a][:, cols].bitcast(E4M3), lhsT_scale=w1_s[a][:, cols],
                            rhs=words, rhs_scale=scales, start=(a == 0 and i == 0), stop=(a == 1 and i == 1),
                        )
                banks.append(bank)
            return banks

        def sines(banks):
            s = work.tile([P, 4, CH], F32, name="s")
            for b in range(2):
                nc.scalar.activation(s[:, 2 * b : 2 * b + 2, :], banks[b][:], ACT.Sin, scale=1.0 / 3.0)
            return s

        def factors(s):
            u = work.tile([P, 4, CH], F32, name="u")
            nc.scalar.activation(u[:], s[:], ACT.Square)
            for t in range(4):
                nc.scalar.activation(
                    u[:, t, :], u[:, t, :], ACT.Identity, scale=g_m4[:, t : t + 1], bias=g_3[:, t : t + 1]
                )
            return u

        def keep_h1(banks, c):
            for t in range(4):
                nc.scalar.copy(h1[t][:, CH * c : CH * (c + 1)], banks[t // 2][:, t % 2, :])

        def quantise_z1(s, u):
            z_g = work.tile([P, 4 * CH], BF16, name="z_g", align_bytes=64)
            z_c = work.tile([P, CH], U32, name="z_c", align_bytes=64)
            z_s = work.tile([P, CH], U8, name="z_s", align_bytes=64)
            nc.vector.tensor_tensor(woven(z_g[:]), planes(u[:]), planes(s[:]), ALU.mult)
            quantise(z_c[:], z_s[:], z_g[:])
            return z_c, z_s

        def stage2(c, z):
            z_c, z_s = z
            banks = []
            for n in range(NT):
                bank = psum.tile([P, 2 * CH], F32, name="y_bank")
                for a in range(2):
                    words, scales = v_operand(a, c)
                    nc.tensor.matmul_mx(
                        out=bank[:, :CH], lhsT=w4_w[:, a, 2 * P * n : 2 * P * (n + 1)].bitcast(E2M1),
                        lhsT_scale=w4_s[:, N * a + P * n : N * a + P * (n + 1)],
                        rhs=words, rhs_scale=scales, start=(a == 0), stop=False,
                    )
                cols = slice(P * n, P * (n + 1))
                nc.tensor.matmul_mx(
                    out=bank[:, :CH], lhsT=w3_c[:, cols].bitcast(E4M3), lhsT_scale=w3_s[:, cols],
                    rhs=z_c[:].bitcast(E4M3), rhs_scale=z_s[:], start=False, stop=True,
                )
                banks.append(bank)
            return banks

        def place1(c, n, bank):
            y = stage.tile([P, CH], F32, name="y")
            if (c, n) == (0, 0):
                nc.vector.tensor_copy(y[:], bank[:, :CH])
            else:
                nc.scalar.copy(y[:], bank[:, :CH])
            gains = wg1_first[:] if c == 0 else wg1_rest[:, CH * (c - 1) : CH * c]
            nc.vector.tensor_tensor(page[n][:].indirect(list_cols(l_offs3, c)), y[:], gains, ALU.mult)

        def stage1_declarations(w2_s):
            for t in range(4):
                bank = psum.tile([P, 2, CH], F32, name="h_bank")
                cols = slice(P * t, P * (t + 1))
                flat = bank[:].rearrange("p i c -> p (i c)")
                nc.tensor.matmul_mx(
                    out=flat, lhsT=w2_c[:, cols].bitcast(E4M3), lhsT_scale=w2_s[:, cols],
                    rhs=v2_w[:].bitcast(E4M3), rhs_scale=v2_s[:], start=True, stop=True,
                )
                nc.scalar.copy(h2[:, t, :], flat)

        last = NCH - 1
        h_banks = stage1(0)
        s = sines(h_banks)
        z = quantise_z1(s, factors(s))
        keep_h1(h_banks, 0)
        y_banks = stage2(0, z)
        for c in range(1, last):
            h_banks = stage1(c)
            s = sines(h_banks)
            place1(c - 1, 0, y_banks[0])
            place1(c - 1, 1, y_banks[1])
            z = quantise_z1(s, factors(s))
            if c == 1:
                w2_s = work.tile([P, H], U8, name="z_g", align_bytes=64)
                nc.vector.tensor_copy(
                    w2_s[:].rearrange("p (t m) -> p t m", t=4), w2_s_raw[:].rearrange("p (m t) -> p t m", t=4)
                )
            place1(c - 1, 2, y_banks[2])
            keep_h1(h_banks, c)
            y_banks = stage2(c, z)

        place1(last - 1, 0, y_banks[0])
        place1(last - 1, 1, y_banks[1])
        stage1_declarations(w2_s)
        h_banks = stage1(last)
        s = sines(h_banks)
        keep_h1(h_banks, last)
        d = kt("d", [P, 4, PN], F32)
        for t in range(4):
            nc.vector.tensor_tensor(d[:, t, :], h1[t][:].indirect(l_pos1[:]), h2[:, t, :], ALU.subtract)
        z = quantise_z1(s, factors(s))
        place1(last - 1, 2, y_banks[2])
        y_banks = stage2(last, z)

        w5_g = kt("w5_g", [P, 4 * N], BF16)
        w5_c = kt("w5_c", [P, N], U32)
        w5_s = kt("w5_s", [P, N], U8)
        nc.scalar.copy(woven(w5_g[:]), planes(w5_raw[:]))
        quantise(w5_c[:], w5_s[:], w5_g[:])

        z2_p = kt("z2_p", [P, 4, PN], BF16)
        for t in range(4):
            nc.scalar.activation(d[:, t, :], d[:, t, :], ACT.Abs)
            nc.scalar.activation(z2_p[:, t, :], d[:, t, :], ACT.Copy, scale=g2_sb[:, t : t + 1])
        place1(last, 0, y_banks[0])
        place1(last, 1, y_banks[1])
        z2_g = kt("z2_g", [P, 4 * PN], BF16)
        z2_c = kt("z2_c", [P, PN], U32)
        z2_s = kt("z2_s", [P, PN], U8)
        nc.scalar.copy(woven(z2_g[:]), planes(z2_p[:]))
        quantise(z2_c[:], z2_s[:], z2_g[:])
        place1(NCH - 1, 2, y_banks[2])

        for n in range(NT):
            bank = psum.tile([P, 2 * CH], F32, name="y_bank")
            cols = slice(P * n, P * (n + 1))
            nc.tensor.matmul_mx(
                out=bank[:], lhsT=w5_c[:, cols].bitcast(E4M3), lhsT_scale=w5_s[:, cols],
                rhs=z2_c[:].bitcast(E4M3), rhs_scale=z2_s[:], start=True, stop=True,
            )
            y2 = work.tile([P, PN], F32, name="y2")
            nc.scalar.copy(y2[:], bank[:])
            nc.vector.tensor_tensor(page[n][:].indirect(l_offs4[:]), y2[:], wg2_sb[:], ALU.mult)
            nc.sync.dma_start(out[P * n : P * (n + 1), :], page[n][:])
